import numpy as np
import ml_dtypes

BF16 = ml_dtypes.bfloat16


def bf(x):
    return np.asarray(x, np.float32).astype(BF16)


def f32(x):
    return np.asarray(x, np.float32)


def f64(x):
    return np.asarray(x).astype(np.float64)


def striped(idx):
    return np.concatenate([l.reshape(-1, 16).T for l in idx])


def rows(idx, k):
    return np.tile(np.repeat(idx, 16, axis=0), (k // (16 * 8), 1))


def look(tab, idx):
    return np.take_along_axis(f64(tab), rows(idx, len(tab)), axis=1)


K, S, H, D, V, N, M = 128, 2048, 256, 2, 1024, 2048, 256


def setup_inputs():
    return {"z": bf(np.random.standard_normal((H, S))), "wt": bf(np.random.standard_normal((H, K)) / np.sqrt(H)), "ctr": f32(1.0 * np.random.standard_normal((K, V))), "w": bf(np.random.standard_normal((K, M)) / np.sqrt(K)), "b": f32(0.5 * np.random.standard_normal((M, 1))), "offs": striped(np.stack([np.random.permutation(S)[:N] for _ in range(8)]))}


def reference(z, wt, ctr, w, b, offs):
    idx = np.stack([g.T.reshape(-1) for g in np.split(offs, 8)])
    tab = f64(wt).T @ f64(z)
    x = sum(np.maximum(look(tab, idx[:, d * V:(d + 1) * V]) - f64(ctr), 0.0) for d in range(D))
    return np.maximum(f64(w).T @ x + f64(b), 0.0)

@@ -1,0 +1,75 @@
+import concourse.mybir as mybir
+
+P = 128
+H = 256
+S = 2048
+V = 1024
+M = 256
+D = 2
+PIECE = 512
+GROUP = 16
+
+FLOPS = 2 * H * P * S + 2 * P * M * V
+
+BF16, F32, U16 = mybir.dt.bfloat16, mybir.dt.float32, mybir.dt.uint16
+ALU = mybir.AluOpType
+RELU = mybir.ActivationFunctionType.Relu
+
+
+def tile_lookup_pjedge_relu_kernel(tc, z, wt, ctr, w, b, offs, out):
+    nc = tc.nc
+    z_rows = z.rearrange("(p h) s -> p h s", h=2)
+    out_rows = out.rearrange("(p h) v -> p h v", h=2)
+
+    with (
+        tc.tile_pool(name="held", bufs=1) as held,
+        tc.psum_pool(name="psum", bufs=1) as psum,
+    ):
+        proj = held.tile([P, 2, P], BF16, name="proj")
+        nc.sync.dma_start(proj[:], wt.rearrange("(p h) r -> p h r", h=2))
+        feats = []
+        for c in range(S // PIECE):
+            feat = held.tile([P, 2, PIECE], BF16, name=f"feat{c}")
+            nc.sync.dma_start(feat[:], z_rows[:, :, c * PIECE:(c + 1) * PIECE])
+            feats.append(feat)
+        offsets = held.tile([P, D * V // GROUP], U16, name="offsets")
+        nc.sync.dma_start(offsets[:], offs)
+        centres = []
+        for c in range(V // PIECE):
+            centre = held.tile([P, PIECE], F32, name=f"centre{c}")
+            nc.sync.dma_start(centre[:], ctr[:, c * PIECE:(c + 1) * PIECE])
+            centres.append(centre)
+        layer = held.tile([P, M], BF16, name="layer")
+        nc.sync.dma_start(layer[:], w)
+        bias = held.tile([P, 2], F32, name="bias")
+        nc.sync.dma_start(bias[:], b.rearrange("(p h) o -> p (h o)", h=2))
+
+        table = held.tile([P, S], F32, name="table")
+        for c, feat in enumerate(feats):
+            bank = psum.tile([P, PIECE], F32, name=f"tab_bank{c}")
+            for h in range(2):
+                nc.tensor.matmul(bank[:], proj[:, h, :], feat[:, h, :], start=(h == 0), stop=(h == 1))
+            cols = table[:, c * PIECE:(c + 1) * PIECE]
+            if c % 2 == 0:
+                nc.scalar.copy(cols, bank[:])
+            else:
+                nc.vector.tensor_copy(cols, bank[:])
+
+        for c, centre in enumerate(centres):
+            diffs = []
+            for d in range(D):
+                first = (d * V + c * PIECE) // GROUP
+                picked = table[:].indirect(offsets[:, first:first + PIECE // GROUP])
+                diff = held.tile([P, PIECE], F32, name=f"diff{c}_{d}")
+                nc.vector.tensor_tensor(diff[:], picked, centre[:], ALU.subtract)
+                diffs.append(diff)
+            part = held.tile([P, PIECE], F32, name=f"part{c}")
+            nc.scalar.activation(part[:], diffs[0][:], RELU)
+            x = held.tile([P, PIECE], BF16, name=f"x{c}")
+            nc.vector.scalar_tensor_tensor(x[:], diffs[1][:], 0.0, part[:], ALU.max, ALU.add)
+            for h in range(2):
+                bank = psum.tile([P, PIECE], F32, name=f"out_bank{c}_{h}")
+                nc.tensor.matmul(bank[:], layer[:, h::2], x[:], start=True, stop=True)
+                res = held.tile([P, PIECE], F32, name=f"res{c}_{h}")
+                nc.scalar.activation(res[:], bank[:], RELU, bias=bias[:, h:h + 1])
+                nc.sync.dma_start(out_rows[:, h, c * PIECE:(c + 1) * PIECE], res[:])

@@ -6,8 +6,11 @@ S = 2048
 V = 1024
 M = 256
 D = 2
-PIECE = 512
 GROUP = 16
+BANK = 512
+SPAN = 1024
+PIECE = 512
+STRIP = 256
 
 FLOPS = 2 * H * P * S + 2 * P * M * V
 
@@ -18,20 +21,20 @@ RELU = mybir.ActivationFunctionType.Relu
 
 def tile_lookup_pjedge_relu_kernel(tc, z, wt, ctr, w, b, offs, out):
     nc = tc.nc
-    z_rows = z.rearrange("(p h) s -> p h s", h=2)
+    z_rows = z.rearrange("(p k) s -> p k s", k=2)
     out_rows = out.rearrange("(p h) v -> p h v", h=2)
 
     with (
         tc.tile_pool(name="held", bufs=1) as held,
-        tc.psum_pool(name="psum", bufs=1) as psum,
+        tc.psum_pool(name="psum", bufs=8) as psum,
     ):
         proj = held.tile([P, 2, P], BF16, name="proj")
-        nc.sync.dma_start(proj[:], wt.rearrange("(p h) r -> p h r", h=2))
-        feats = []
-        for c in range(S // PIECE):
-            feat = held.tile([P, 2, PIECE], BF16, name=f"feat{c}")
-            nc.sync.dma_start(feat[:], z_rows[:, :, c * PIECE:(c + 1) * PIECE])
-            feats.append(feat)
+        nc.scalar.dma_start(proj[:], wt.rearrange("(p k) r -> p k r", k=2))
+        feats = {}
+        for s in range(S // SPAN):
+            for k in range(2):
+                feats[s, k] = held.tile([P, SPAN], BF16, name=f"feat{s}_{k}")
+                nc.sync.dma_start(feats[s, k][:], z_rows[:, k, s * SPAN:(s + 1) * SPAN])
         offsets = held.tile([P, D * V // GROUP], U16, name="offsets")
         nc.sync.dma_start(offsets[:], offs)
         centres = []
@@ -45,15 +48,14 @@ def tile_lookup_pjedge_relu_kernel(tc, z, wt, ctr, w, b, offs, out):
         nc.sync.dma_start(bias[:], b.rearrange("(p h) o -> p (h o)", h=2))
 
         table = held.tile([P, S], F32, name="table")
-        for c, feat in enumerate(feats):
-            bank = psum.tile([P, PIECE], F32, name=f"tab_bank{c}")
-            for h in range(2):
-                nc.tensor.matmul(bank[:], proj[:, h, :], feat[:, h, :], start=(h == 0), stop=(h == 1))
-            cols = table[:, c * PIECE:(c + 1) * PIECE]
-            if c % 2 == 0:
-                nc.scalar.copy(cols, bank[:])
-            else:
-                nc.vector.tensor_copy(cols, bank[:])
+        for s in range(S // SPAN):
+            banks = [psum.tile([P, BANK], F32, name="bank") for i in range(2)]
+            for k in range(2):
+                for i in range(2):
+                    nc.tensor.matmul(banks[i][:], proj[:, k, :], feats[s, k][:, i * BANK:(i + 1) * BANK],
+                                     start=(k == 0), stop=(k == 1))
+            nc.scalar.copy(table[:, s * SPAN:s * SPAN + BANK], banks[0][:])
+            nc.vector.tensor_copy(table[:, s * SPAN + BANK:(s + 1) * SPAN], banks[1][:])
 
         for c, centre in enumerate(centres):
             diffs = []
@@ -65,11 +67,21 @@ def tile_lookup_pjedge_relu_kernel(tc, z, wt, ctr, w, b, offs, out):
                 diffs.append(diff)
             part = held.tile([P, PIECE], F32, name=f"part{c}")
             nc.scalar.activation(part[:], diffs[0][:], RELU)
-            x = held.tile([P, PIECE], BF16, name=f"x{c}")
-            nc.vector.scalar_tensor_tensor(x[:], diffs[1][:], 0.0, part[:], ALU.max, ALU.add)
-            for h in range(2):
-                bank = psum.tile([P, PIECE], F32, name=f"out_bank{c}_{h}")
-                nc.tensor.matmul(bank[:], layer[:, h::2], x[:], start=True, stop=True)
-                res = held.tile([P, PIECE], F32, name=f"res{c}_{h}")
-                nc.scalar.activation(res[:], bank[:], RELU, bias=bias[:, h:h + 1])
-                nc.sync.dma_start(out_rows[:, h, c * PIECE:(c + 1) * PIECE], res[:])
+            strips = [slice(t * STRIP, (t + 1) * STRIP) for t in range(PIECE // STRIP)]
+            xs = []
+            for t, cols in enumerate(strips):
+                x = held.tile([P, STRIP], BF16, name=f"x{c}_{t}")
+                nc.vector.scalar_tensor_tensor(x[:], diffs[1][:, cols], 0.0, part[:, cols], ALU.max, ALU.add)
+                xs.append(x)
+            look_ups_left = c + 1 < len(centres)
+            for t, x in enumerate(xs):
+                res = held.tile([P, 2, STRIP], F32, name=f"res{c}_{t}")
+                for h in range(2):
+                    bank = psum.tile([P, STRIP], F32, name="bank")
+                    nc.tensor.matmul(bank[:], layer[:, h::2], x[:], start=True, stop=True)
+                    if look_ups_left or h == 0:
+                        nc.scalar.activation(res[:, h, :], bank[:], RELU, bias=bias[:, h:h + 1])
+                    else:
+                        nc.vector.tensor_scalar(res[:, h, :], bank[:], bias[:, h:h + 1], 0.0, ALU.add, ALU.max)
+                start = c * PIECE + t * STRIP
+                nc.sync.dma_start(out_rows[:, :, start:start + STRIP], res[:])

@@ -7,10 +7,10 @@ V = 1024
 M = 256
 D = 2
 GROUP = 16
-BANK = 512
 SPAN = 1024
 PIECE = 512
 STRIP = 256
+WARM = 12
 
 FLOPS = 2 * H * P * S + 2 * P * M * V
 
@@ -47,15 +47,25 @@ def tile_lookup_pjedge_relu_kernel(tc, z, wt, ctr, w, b, offs, out):
         bias = held.tile([P, 2], F32, name="bias")
         nc.sync.dma_start(bias[:], b.rearrange("(p h) o -> p (h o)", h=2))
 
+        zeros = held.tile([P, P], BF16, name="zeros")
+        nc.vector.memset(zeros[:], 0.0)
+        idle = psum.tile([P, P], F32, name="bank")
+        for i in range(WARM):
+            nc.tensor.matmul(idle[:], zeros[:], zeros[:], start=True, stop=True)
+
         table = held.tile([P, S], F32, name="table")
         for s in range(S // SPAN):
-            banks = [psum.tile([P, BANK], F32, name="bank") for i in range(2)]
+            banks = [psum.tile([P, STRIP], F32, name="bank") for t in range(SPAN // STRIP)]
             for k in range(2):
-                for i in range(2):
-                    nc.tensor.matmul(banks[i][:], proj[:, k, :], feats[s, k][:, i * BANK:(i + 1) * BANK],
+                for t, bank in enumerate(banks):
+                    nc.tensor.matmul(bank[:], proj[:, k, :], feats[s, k][:, t * STRIP:(t + 1) * STRIP],
                                      start=(k == 0), stop=(k == 1))
-            nc.scalar.copy(table[:, s * SPAN:s * SPAN + BANK], banks[0][:])
-            nc.vector.tensor_copy(table[:, s * SPAN + BANK:(s + 1) * SPAN], banks[1][:])
+            for t, bank in enumerate(banks):
+                cols = table[:, s * SPAN + t * STRIP:s * SPAN + (t + 1) * STRIP]
+                if t % 2 == 0:
+                    nc.scalar.copy(cols, bank[:])
+                else:
+                    nc.vector.tensor_copy(cols, bank[:])
 
         for c, centre in enumerate(centres):
             diffs = []

@@ -34,7 +34,10 @@ def tile_lookup_pjedge_relu_kernel(tc, z, wt, ctr, w, b, offs, out):
         for s in range(S // SPAN):
             for k in range(2):
                 feats[s, k] = held.tile([P, SPAN], BF16, name=f"feat{s}_{k}")
-                nc.sync.dma_start(feats[s, k][:], z_rows[:, k, s * SPAN:(s + 1) * SPAN])
+                width = SPAN // (k + 1)
+                for first in range(0, SPAN, width):
+                    nc.sync.dma_start(feats[s, k][:, first:first + width],
+                                      z_rows[:, k, s * SPAN + first:s * SPAN + first + width])
         offsets = held.tile([P, D * V // GROUP], U16, name="offsets")
         nc.sync.dma_start(offsets[:], offs)
         centres = []
@@ -85,13 +88,13 @@ def tile_lookup_pjedge_relu_kernel(tc, z, wt, ctr, w, b, offs, out):
                 xs.append(x)
             look_ups_left = c + 1 < len(centres)
             for t, x in enumerate(xs):
-                res = held.tile([P, 2, STRIP], F32, name=f"res{c}_{t}")
+                start = c * PIECE + t * STRIP
                 for h in range(2):
                     bank = psum.tile([P, STRIP], F32, name="bank")
                     nc.tensor.matmul(bank[:], layer[:, h::2], x[:], start=True, stop=True)
+                    res = held.tile([P, STRIP], F32, name=f"res{c}_{t}_{h}")
                     if look_ups_left or h == 0:
-                        nc.scalar.activation(res[:, h, :], bank[:], RELU, bias=bias[:, h:h + 1])
+                        nc.scalar.activation(res[:], bank[:], RELU, bias=bias[:, h:h + 1])
                     else:
-                        nc.vector.tensor_scalar(res[:, h, :], bank[:], bias[:, h:h + 1], 0.0, ALU.add, ALU.max)
-                start = c * PIECE + t * STRIP
-                nc.sync.dma_start(out_rows[:, :, start:start + STRIP], res[:])
+                        nc.vector.tensor_scalar(res[:], bank[:], bias[:, h:h + 1], 0.0, ALU.add, ALU.max)
+                    nc.sync.dma_start(out_rows[:, h, start:start + STRIP], res[:])

import concourse.mybir as mybir

P = 128
H = 256
S = 2048
V = 1024
M = 256
D = 2
GROUP = 16
SPAN = 1024
PIECE = 512
STRIP = 256
WARM = 12

FLOPS = 2 * H * P * S + 2 * P * M * V

BF16, F32, U16 = mybir.dt.bfloat16, mybir.dt.float32, mybir.dt.uint16
ALU = mybir.AluOpType
RELU = mybir.ActivationFunctionType.Relu


def tile_lookup_pjedge_relu_kernel(tc, z, wt, ctr, w, b, offs, out):
    nc = tc.nc
    z_rows = z.rearrange("(p k) s -> p k s", k=2)
    out_rows = out.rearrange("(p h) v -> p h v", h=2)

    with (
        tc.tile_pool(name="held", bufs=1) as held,
        tc.psum_pool(name="psum", bufs=8) as psum,
    ):
        proj = held.tile([P, 2, P], BF16, name="proj")
        nc.scalar.dma_start(proj[:], wt.rearrange("(p k) r -> p k r", k=2))
        feats = {}
        for s in range(S // SPAN):
            for k in range(2):
                feats[s, k] = held.tile([P, SPAN], BF16, name=f"feat{s}_{k}")
                width = SPAN // (k + 1)
                for first in range(0, SPAN, width):
                    nc.sync.dma_start(feats[s, k][:, first:first + width],
                                      z_rows[:, k, s * SPAN + first:s * SPAN + first + width])
        offsets = held.tile([P, D * V // GROUP], U16, name="offsets")
        nc.sync.dma_start(offsets[:], offs)
        centres = []
        for c in range(V // PIECE):
            centre = held.tile([P, PIECE], F32, name=f"centre{c}")
            nc.sync.dma_start(centre[:], ctr[:, c * PIECE:(c + 1) * PIECE])
            centres.append(centre)
        layer = held.tile([P, M], BF16, name="layer")
        nc.sync.dma_start(layer[:], w)
        bias = held.tile([P, 2], F32, name="bias")
        nc.sync.dma_start(bias[:], b.rearrange("(p h) o -> p (h o)", h=2))

        zeros = held.tile([P, P], BF16, name="zeros")
        nc.vector.memset(zeros[:], 0.0)
        idle = psum.tile([P, P], F32, name="bank")
        for i in range(WARM):
            nc.tensor.matmul(idle[:], zeros[:], zeros[:], start=True, stop=True)

        table = held.tile([P, S], F32, name="table")
        for s in range(S // SPAN):
            banks = [psum.tile([P, STRIP], F32, name="bank") for t in range(SPAN // STRIP)]
            for k in range(2):
                for t, bank in enumerate(banks):
                    nc.tensor.matmul(bank[:], proj[:, k, :], feats[s, k][:, t * STRIP:(t + 1) * STRIP],
                                     start=(k == 0), stop=(k == 1))
            for t, bank in enumerate(banks):
                cols = table[:, s * SPAN + t * STRIP:s * SPAN + (t + 1) * STRIP]
                if t % 2 == 0:
                    nc.scalar.copy(cols, bank[:])
                else:
                    nc.vector.tensor_copy(cols, bank[:])

        for c, centre in enumerate(centres):
            diffs = []
            for d in range(D):
                first = (d * V + c * PIECE) // GROUP
                picked = table[:].indirect(offsets[:, first:first + PIECE // GROUP])
                diff = held.tile([P, PIECE], F32, name=f"diff{c}_{d}")
                nc.vector.tensor_tensor(diff[:], picked, centre[:], ALU.subtract)
                diffs.append(diff)
            part = held.tile([P, PIECE], F32, name=f"part{c}")
            nc.scalar.activation(part[:], diffs[0][:], RELU)
            strips = [slice(t * STRIP, (t + 1) * STRIP) for t in range(PIECE // STRIP)]
            xs = []
            for t, cols in enumerate(strips):
                x = held.tile([P, STRIP], BF16, name=f"x{c}_{t}")
                nc.vector.scalar_tensor_tensor(x[:], diffs[1][:, cols], 0.0, part[:, cols], ALU.max, ALU.add)
                xs.append(x)
            look_ups_left = c + 1 < len(centres)
            for t, x in enumerate(xs):
                start = c * PIECE + t * STRIP
                for h in range(2):
                    bank = psum.tile([P, STRIP], F32, name="bank")
                    nc.tensor.matmul(bank[:], layer[:, h::2], x[:], start=True, stop=True)
                    res = held.tile([P, STRIP], F32, name=f"res{c}_{t}_{h}")
                    if look_ups_left or h == 0:
                        nc.scalar.activation(res[:], bank[:], RELU, bias=bias[:, h:h + 1])
                    else:
                        nc.vector.tensor_scalar(res[:], bank[:], bias[:, h:h + 1], 0.0, ALU.add, ALU.max)
                    nc.sync.dma_start(out_rows[:, h, start:start + STRIP], res[:])
